import numpy as np
import ml_dtypes

BF16 = ml_dtypes.bfloat16


def bf(x):
    return np.asarray(x, np.float32).astype(BF16)


def f32(x):
    return np.asarray(x, np.float32)


def f64(x):
    return np.asarray(x).astype(np.float64)


def striped(idx):
    return np.tile(idx.reshape(-1, 16).T, (8, 1))


S, K, M, N, E, Q = 512, 128, 512, 256, 4, 64


def setup_inputs():
    return {"base": bf(np.random.standard_normal((M, S))), "x": bf(np.random.standard_normal((K, N))), "w": bf(np.random.standard_normal((E, K, M)) / np.sqrt(K)), "s": f32(0.5 + np.random.random_sample((M, 1))), "b": f32(0.5 * np.random.standard_normal((M, 1))), "offs": striped(np.random.permutation(S)[:N])}


def reference(base, x, w, s, b, offs):
    idx = offs[:16].T.reshape(-1)
    z = f64(base).copy()
    for e in range(E):
        z[:, idx[e * Q : (e + 1) * Q]] += f64(w)[e].T @ f64(x)[:, e * Q : (e + 1) * Q]
    return z * f64(s) + f64(b)

@@ -1,0 +1,69 @@
+import concourse.mybir as mybir
+from concourse.masks import make_identity
+
+FEATURES = 512
+TOKENS = 512
+K = 128
+EXPERTS = 4
+PIECE = 64
+ENTRIES = EXPERTS * PIECE
+P = 128
+BLOCKS = FEATURES // P
+LANES = 16
+
+FLOPS = 2 * K * FEATURES * ENTRIES
+
+F32, BF16, U16 = mybir.dt.float32, mybir.dt.bfloat16, mybir.dt.uint16
+MULT, ADD = mybir.AluOpType.mult, mybir.AluOpType.add
+IDENTITY = mybir.ActivationFunctionType.Identity
+
+
+def tile_scatter_matmul_kernel(tc, base, x, w, s, b, offs, out):
+    nc = tc.nc
+    with (
+        tc.tile_pool(name="held", bufs=1) as held,
+        tc.psum_pool(name="windows", bufs=1) as psum,
+    ):
+        base_rows = base.rearrange("(a p) t -> p a t", p=P)
+        base_tile = held.tile([P, BLOCKS, TOKENS], BF16, name="base_tile")
+        for half in range(2):
+            blocks = slice(half * BLOCKS // 2, (half + 1) * BLOCKS // 2)
+            nc.sync.dma_start(base_tile[:, blocks, :], base_rows[:, blocks, :])
+
+        offsets = held.tile([P, ENTRIES // LANES], U16, name="offsets")
+        nc.sync.dma_start(offsets[:], offs)
+
+        x_tile = held.tile([P, ENTRIES], BF16, name="x_tile")
+        nc.sync.dma_start(x_tile[:], x)
+
+        w_rows = w.rearrange("e k m -> k e m")
+        w_tile = held.tile([P, EXPERTS, FEATURES], BF16, name="w_tile")
+        for half in range(2):
+            experts = slice(half * EXPERTS // 2, (half + 1) * EXPERTS // 2)
+            nc.sync.dma_start(w_tile[:, experts, :], w_rows[:, experts, :])
+
+        gain = held.tile([P, BLOCKS], F32, name="gain")
+        nc.sync.dma_start(gain[:], s.rearrange("(a p) o -> p (a o)", p=P))
+        shift = held.tile([P, BLOCKS], F32, name="shift")
+        nc.sync.dma_start(shift[:], b.rearrange("(a p) o -> p (a o)", p=P))
+
+        ident = held.tile([P, P], BF16, name="ident")
+        make_identity(nc, ident[:])
+        windows = [psum.tile([P, TOKENS], F32, name=f"window{a}") for a in range(BLOCKS)]
+        for a in range(BLOCKS):
+            nc.tensor.matmul(windows[a][:], ident[:], base_tile[:, a, :], start=True, stop=False)
+
+        for e in range(EXPERTS):
+            piece = offsets[:, e * PIECE // LANES : (e + 1) * PIECE // LANES]
+            moving = x_tile[:, e * PIECE : (e + 1) * PIECE]
+            for a in range(BLOCKS):
+                weights = w_tile[:, e, a * P : (a + 1) * P]
+                nc.tensor.matmul(windows[a][:].indirect(piece), weights, moving, start=False, stop=e == EXPERTS - 1)
+
+        for a in range(BLOCKS):
+            result = held.tile([P, TOKENS], F32, name=f"result{a}")
+            if a % 2 == 0:
+                nc.vector.tensor_scalar(result[:], windows[a][:], gain[:, a : a + 1], shift[:, a : a + 1], MULT, ADD)
+            else:
+                nc.scalar.activation(result[:], windows[a][:], IDENTITY, bias=shift[:, a : a + 1], scale=gain[:, a : a + 1])
+            nc.sync.dma_start(out[a * P : (a + 1) * P, :], result[:])

@@ -24,7 +24,8 @@ def tile_scatter_matmul_kernel(tc, base, x, w, s, b, offs, out):
         tc.tile_pool(name="held", bufs=1) as held,
         tc.psum_pool(name="windows", bufs=1) as psum,
     ):
-        base_rows = base.rearrange("(a p) t -> p a t", p=P)
+        base_rows = base.rearrange("(p a) t -> p a t", p=P)
+        out_rows = out.rearrange("(p a) t -> p a t", p=P)
         base_tile = held.tile([P, BLOCKS, TOKENS], BF16, name="base_tile")
         for half in range(2):
             blocks = slice(half * BLOCKS // 2, (half + 1) * BLOCKS // 2)
@@ -43,9 +44,9 @@ def tile_scatter_matmul_kernel(tc, base, x, w, s, b, offs, out):
             nc.sync.dma_start(w_tile[:, experts, :], w_rows[:, experts, :])
 
         gain = held.tile([P, BLOCKS], F32, name="gain")
-        nc.sync.dma_start(gain[:], s.rearrange("(a p) o -> p (a o)", p=P))
+        nc.sync.dma_start(gain[:], s.rearrange("(p a) o -> p (a o)", p=P))
         shift = held.tile([P, BLOCKS], F32, name="shift")
-        nc.sync.dma_start(shift[:], b.rearrange("(a p) o -> p (a o)", p=P))
+        nc.sync.dma_start(shift[:], b.rearrange("(p a) o -> p (a o)", p=P))
 
         ident = held.tile([P, P], BF16, name="ident")
         make_identity(nc, ident[:])
@@ -53,12 +54,13 @@ def tile_scatter_matmul_kernel(tc, base, x, w, s, b, offs, out):
         for a in range(BLOCKS):
             nc.tensor.matmul(windows[a][:], ident[:], base_tile[:, a, :], start=True, stop=False)
 
-        for e in range(EXPERTS):
-            piece = offsets[:, e * PIECE // LANES : (e + 1) * PIECE // LANES]
-            moving = x_tile[:, e * PIECE : (e + 1) * PIECE]
+        for half in range(2):
             for a in range(BLOCKS):
-                weights = w_tile[:, e, a * P : (a + 1) * P]
-                nc.tensor.matmul(windows[a][:].indirect(piece), weights, moving, start=False, stop=e == EXPERTS - 1)
+                for e in range(half * EXPERTS // 2, (half + 1) * EXPERTS // 2):
+                    piece = offsets[:, e * PIECE // LANES : (e + 1) * PIECE // LANES]
+                    moving = x_tile[:, e * PIECE : (e + 1) * PIECE]
+                    weights = w_tile[:, e, a::BLOCKS]
+                    nc.tensor.matmul(windows[a][:].indirect(piece), weights, moving, start=False, stop=e == EXPERTS - 1)
 
         for a in range(BLOCKS):
             result = held.tile([P, TOKENS], F32, name=f"result{a}")
@@ -66,4 +68,4 @@ def tile_scatter_matmul_kernel(tc, base, x, w, s, b, offs, out):
                 nc.vector.tensor_scalar(result[:], windows[a][:], gain[:, a : a + 1], shift[:, a : a + 1], MULT, ADD)
             else:
                 nc.scalar.activation(result[:], windows[a][:], IDENTITY, bias=shift[:, a : a + 1], scale=gain[:, a : a + 1])
-            nc.sync.dma_start(out[a * P : (a + 1) * P, :], result[:])
+            nc.sync.dma_start(out_rows[:, a, :], result[:])

@@ -10,6 +10,7 @@ ENTRIES = EXPERTS * PIECE
 P = 128
 BLOCKS = FEATURES // P
 LANES = 16
+WARM_UPS = 4
 
 FLOPS = 2 * K * FEATURES * ENTRIES
 
@@ -24,6 +25,14 @@ def tile_scatter_matmul_kernel(tc, base, x, w, s, b, offs, out):
         tc.tile_pool(name="held", bufs=1) as held,
         tc.psum_pool(name="windows", bufs=1) as psum,
     ):
+        zeros = held.tile([P, TOKENS], BF16, name="zeros")
+        nc.vector.memset(zeros[:], 0.0)
+        first = held.tile([P, 1], F32, name="first")
+        nc.scalar.activation(first[:], zeros[:, 0:1], IDENTITY)
+        spare = psum.tile([P, TOKENS], F32, name="spare")
+        for i in range(WARM_UPS):
+            nc.tensor.matmul(spare[:], zeros[:, 0:P], zeros[:], start=True, stop=True)
+
         base_rows = base.rearrange("(p a) t -> p a t", p=P)
         out_rows = out.rearrange("(p a) t -> p a t", p=P)
         base_tile = held.tile([P, BLOCKS, TOKENS], BF16, name="base_tile")

@@ -63,17 +63,16 @@ def tile_scatter_matmul_kernel(tc, base, x, w, s, b, offs, out):
         for a in range(BLOCKS):
             nc.tensor.matmul(windows[a][:], ident[:], base_tile[:, a, :], start=True, stop=False)
 
-        for half in range(2):
-            for a in range(BLOCKS):
-                for e in range(half * EXPERTS // 2, (half + 1) * EXPERTS // 2):
-                    piece = offsets[:, e * PIECE // LANES : (e + 1) * PIECE // LANES]
-                    moving = x_tile[:, e * PIECE : (e + 1) * PIECE]
-                    weights = w_tile[:, e, a::BLOCKS]
-                    nc.tensor.matmul(windows[a][:].indirect(piece), weights, moving, start=False, stop=e == EXPERTS - 1)
+        for a in range(BLOCKS):
+            for e in range(EXPERTS):
+                piece = offsets[:, e * PIECE // LANES : (e + 1) * PIECE // LANES]
+                moving = x_tile[:, e * PIECE : (e + 1) * PIECE]
+                weights = w_tile[:, e, a::BLOCKS]
+                nc.tensor.matmul(windows[a][:].indirect(piece), weights, moving, start=False, stop=e == EXPERTS - 1)
 
         for a in range(BLOCKS):
             result = held.tile([P, TOKENS], F32, name=f"result{a}")
-            if a % 2 == 0:
+            if a % 2 == 1:
                 nc.vector.tensor_scalar(result[:], windows[a][:], gain[:, a : a + 1], shift[:, a : a + 1], MULT, ADD)
             else:
                 nc.scalar.activation(result[:], windows[a][:], IDENTITY, bias=shift[:, a : a + 1], scale=gain[:, a : a + 1])

import concourse.mybir as mybir
from concourse.masks import make_identity

FEATURES = 512
TOKENS = 512
K = 128
EXPERTS = 4
PIECE = 64
ENTRIES = EXPERTS * PIECE
P = 128
BLOCKS = FEATURES // P
LANES = 16
WARM_UPS = 4

FLOPS = 2 * K * FEATURES * ENTRIES

F32, BF16, U16 = mybir.dt.float32, mybir.dt.bfloat16, mybir.dt.uint16
MULT, ADD = mybir.AluOpType.mult, mybir.AluOpType.add
IDENTITY = mybir.ActivationFunctionType.Identity


def tile_scatter_matmul_kernel(tc, base, x, w, s, b, offs, out):
    nc = tc.nc
    with (
        tc.tile_pool(name="held", bufs=1) as held,
        tc.psum_pool(name="windows", bufs=1) as psum,
    ):
        zeros = held.tile([P, TOKENS], BF16, name="zeros")
        nc.vector.memset(zeros[:], 0.0)
        first = held.tile([P, 1], F32, name="first")
        nc.scalar.activation(first[:], zeros[:, 0:1], IDENTITY)
        spare = psum.tile([P, TOKENS], F32, name="spare")
        for i in range(WARM_UPS):
            nc.tensor.matmul(spare[:], zeros[:, 0:P], zeros[:], start=True, stop=True)

        base_rows = base.rearrange("(p a) t -> p a t", p=P)
        out_rows = out.rearrange("(p a) t -> p a t", p=P)
        base_tile = held.tile([P, BLOCKS, TOKENS], BF16, name="base_tile")
        for half in range(2):
            blocks = slice(half * BLOCKS // 2, (half + 1) * BLOCKS // 2)
            nc.sync.dma_start(base_tile[:, blocks, :], base_rows[:, blocks, :])

        offsets = held.tile([P, ENTRIES // LANES], U16, name="offsets")
        nc.sync.dma_start(offsets[:], offs)

        x_tile = held.tile([P, ENTRIES], BF16, name="x_tile")
        nc.sync.dma_start(x_tile[:], x)

        w_rows = w.rearrange("e k m -> k e m")
        w_tile = held.tile([P, EXPERTS, FEATURES], BF16, name="w_tile")
        for half in range(2):
            experts = slice(half * EXPERTS // 2, (half + 1) * EXPERTS // 2)
            nc.sync.dma_start(w_tile[:, experts, :], w_rows[:, experts, :])

        gain = held.tile([P, BLOCKS], F32, name="gain")
        nc.sync.dma_start(gain[:], s.rearrange("(p a) o -> p (a o)", p=P))
        shift = held.tile([P, BLOCKS], F32, name="shift")
        nc.sync.dma_start(shift[:], b.rearrange("(p a) o -> p (a o)", p=P))

        ident = held.tile([P, P], BF16, name="ident")
        make_identity(nc, ident[:])
        windows = [psum.tile([P, TOKENS], F32, name=f"window{a}") for a in range(BLOCKS)]
        for a in range(BLOCKS):
            nc.tensor.matmul(windows[a][:], ident[:], base_tile[:, a, :], start=True, stop=False)

        for a in range(BLOCKS):
            for e in range(EXPERTS):
                piece = offsets[:, e * PIECE // LANES : (e + 1) * PIECE // LANES]
                moving = x_tile[:, e * PIECE : (e + 1) * PIECE]
                weights = w_tile[:, e, a::BLOCKS]
                nc.tensor.matmul(windows[a][:].indirect(piece), weights, moving, start=False, stop=e == EXPERTS - 1)

        for a in range(BLOCKS):
            result = held.tile([P, TOKENS], F32, name=f"result{a}")
            if a % 2 == 1:
                nc.vector.tensor_scalar(result[:], windows[a][:], gain[:, a : a + 1], shift[:, a : a + 1], MULT, ADD)
            else:
                nc.scalar.activation(result[:], windows[a][:], IDENTITY, bias=shift[:, a : a + 1], scale=gain[:, a : a + 1])
            nc.sync.dma_start(out_rows[:, a, :], result[:])
